import numpy as np
import ml_dtypes


def mxq(x, axis, fmt="e4m3"):
    dtype, down = {"e4m3": (ml_dtypes.float8_e4m3fn, 7), "e5m2": (ml_dtypes.float8_e5m2, 14)}[fmt]
    v = np.moveaxis(np.asarray(x, np.float32).astype(ml_dtypes.bfloat16).astype(np.float64), axis, -1)
    blocks = v.reshape(v.shape[:-1] + (-1, 32))
    amax = np.abs(blocks).max(-1, keepdims=True)
    byte = np.maximum(np.where(amax > 0, np.frexp(amax)[1] - 1 + 127, 0) - down, 1)
    scale = np.exp2(byte - 127.0)
    codes = (blocks / scale).astype(np.float32).astype(dtype).astype(np.float64)
    return np.moveaxis((codes * scale).reshape(v.shape), -1, axis)


WIDE = False


def mx_kscale(k):
    if not WIDE:
        return np.ones(k)
    levels = np.array([10, -10, 5, -5, 0])
    if k % 512:
        return np.exp2(np.random.permutation(np.resize(levels, k // 32))).repeat(32)
    a = np.empty((k // 512, 16))
    for p in range(k // 512):
        a[p, :8] = np.random.permutation(np.resize(levels, 8))
        for g in range(8):
            far = levels[np.abs(levels - a[p, g]) >= 10]
            a[p, g + 8] = far[np.random.randint(len(far))]
    return np.exp2(a.ravel()).repeat(32)


def f64(x):
    return np.asarray(x).astype(np.float64)


def striped(idx):
    return np.tile(idx.reshape(-1, 16).T, (8, 1)).astype(np.uint16)


def unstriped(offs):
    return offs[:16].T.reshape(-1).astype(np.int64)


E2M1 = np.array([0.0, 0.5, 1.0, 1.5, 2.0, 3.0, 4.0, 6.0, -0.0, -0.5, -1.0, -1.5, -2.0, -3.0, -4.0, -6.0])


def pack_weight(w, fmt):
    k, n = w.shape
    w = f64(np.asarray(w, np.float32).astype(ml_dtypes.bfloat16)).reshape(k // 32, 32, n)
    amax = np.abs(w).max(1)
    if fmt == "e4m3":
        byte = np.frexp(amax)[1] - 1 + 127 - 7
    else:
        mant, ex = np.frexp(amax / 6.0)
        byte = np.where(mant > 0.5, ex, ex - 1) + 127
    byte = np.clip(np.where(amax > 0, byte, 1), 1, 254)
    scaled = (w * np.exp2(127.0 - byte)[:, None, :]).reshape(k, n).astype(np.float32)
    by_word = np.ascontiguousarray(scaled.reshape(k // 512, 128, 4, n).transpose(0, 1, 3, 2))
    if fmt == "e4m3":
        words = by_word.astype(ml_dtypes.float8_e4m3fn).view(np.uint8)
    else:
        c = by_word.astype(ml_dtypes.float4_e2m1fn).view(np.uint8) & 0xF
        words = (c[..., 0::2] | (c[..., 1::2] << 4)).reshape(k // 512, 128, 2 * n)
    return np.ascontiguousarray(words), np.ascontiguousarray(byte.astype(np.uint8).reshape(k // 512, 16, n))


def unpack_weight(words, scales, fmt):
    g, _, n = scales.shape
    words = np.ascontiguousarray(words).reshape(g, 128, n, -1)
    if fmt == "e4m3":
        vals = words.view(ml_dtypes.float8_e4m3fn).astype(np.float64)
    else:
        nib = np.empty((g, 128, n, 4), np.uint8)
        nib[..., 0::2] = words & 0xF
        nib[..., 1::2] = words >> 4
        vals = E2M1[nib]
    vals = vals * np.repeat(np.exp2(scales.astype(np.float64) - 127.0), 8, axis=1)[..., None]
    return vals.transpose(0, 1, 3, 2).reshape(g * 512, n)


def relu(v):
    return np.maximum(v, 0.0)


K, T, E, C, H, N = 512, 1024, 4, 128, 1024, 128


def by_expert(wq, xq):
    return np.concatenate([wq[e].T @ xq[:, e * C:(e + 1) * C] for e in range(E)], axis=1)


def setup_inputs():
    n = np.random.standard_normal
    s = mx_kscale(K)[:, None]
    u = mx_kscale(H)
    w1 = [pack_weight(m, "e2m1") for m in n((E, K, H)) / np.sqrt(K) / s[None]]
    w3 = [pack_weight(m, "e2m1") for m in n((E, K, H)) / np.sqrt(K) / s[None] * u[None, None, :]]
    w2 = [pack_weight(m, "e2m1") for m in n((E, H, N)) / np.sqrt(H) / u[None, :, None]]
    return {
        "xT": (n((K, T)) * s).astype(np.float32),
        "w1_words": np.stack([m[0] for m in w1]),
        "w1_scales": np.stack([m[1] for m in w1]),
        "w3_words": np.stack([m[0] for m in w3]),
        "w3_scales": np.stack([m[1] for m in w3]),
        "w2_words": np.stack([m[0] for m in w2]),
        "w2_scales": np.stack([m[1] for m in w2]),
        "gate": np.tile(np.random.uniform(0.2, 1.0, E * C), (N, 1)).astype(np.float32),
        "offs": striped(np.random.permutation(T)[:E * C]),
        "dst": striped(np.random.permutation(T)[:E * C]),
    }


def reference(xT, w1_words, w1_scales, w3_words, w3_scales, w2_words, w2_scales, gate, offs, dst):
    idx = unstriped(offs)
    w1 = np.stack([unpack_weight(w1_words[e], w1_scales[e], "e2m1") for e in range(E)])
    w3 = np.stack([unpack_weight(w3_words[e], w3_scales[e], "e2m1") for e in range(E)])
    w2 = np.stack([unpack_weight(w2_words[e], w2_scales[e], "e2m1") for e in range(E)])
    xq = mxq(f64(xT)[:, idx], 0, "e4m3")
    h = relu(by_expert(w1, xq))
    h = h * by_expert(w3, xq)
    y = by_expert(w2, mxq(h, 0, "e4m3"))
    out = np.zeros((N, T))
    out[:, unstriped(dst)] = f64(gate) * y
    return out

@@ -1,0 +1,191 @@
+from contextlib import ExitStack
+
+import concourse.mybir as mybir
+from concourse.masks import make_identity
+
+K, T, E, C, H, N = 512, 1024, 4, 128, 1024, 128
+P = 128
+FLOPS = 2 * E * C * (2 * K * H + H * N)
+
+F32 = mybir.dt.float32
+BF16 = mybir.dt.bfloat16
+I32 = mybir.dt.int32
+U32 = mybir.dt.uint32
+U16 = mybir.dt.uint16
+U8 = mybir.dt.uint8
+FP8X4 = mybir.dt.float8_e4m3fn_x4
+FP4X4 = mybir.dt.float4_e2m1fn_x4
+MULT = mybir.AluOpType.mult
+RELU = mybir.ActivationFunctionType.Relu
+
+HALF = 512
+PASSES = H // HALF
+
+
+def tile_moe_two_glu_relu_kernel(tc, xT, w1_words, w1_scales, w3_words, w3_scales, w2_words, w2_scales, gate, offs, dst, out):
+    nc = tc.nc
+    with ExitStack() as ctx:
+        keep = ctx.enter_context(tc.tile_pool(name="keep", bufs=1))
+        work = ctx.enter_context(tc.tile_pool(name="work", bufs=3))
+        psum_ab = ctx.enter_context(tc.psum_pool(name="psum_ab", bufs=2))
+        psum_t = ctx.enter_context(tc.psum_pool(name="psum_t", bufs=2))
+        psum_y = ctx.enter_context(tc.psum_pool(name="psum_y", bufs=2))
+
+        offsets = keep.tile([P, E * C // 16], U16, name="offsets")
+        nc.sync.dma_start(offsets[:], offs)
+        xv = xT.rearrange("(p t) n -> p t n", t=4)
+        planes = []
+        for t in range(4):
+            plane = keep.tile([P, T], F32, name="plane%d" % t)
+            nc.sync.dma_start(plane[:], xv[:, t, :])
+            planes.append(plane)
+
+        s1 = keep.tile([P, E, H], U8, name="s1", align_bytes=64)
+        s3 = keep.tile([P, E, H], U8, name="s3", align_bytes=64)
+        s2 = keep.tile([P, E * PASSES, N], U8, name="s2", align_bytes=64)
+        s1w, s3w, s2w = s1[:].bitcast(I32), s3[:].bitcast(I32), s2[:].bitcast(I32)
+        nc.vector.memset(s1w[:, 0:1, :], 0)
+        nc.vector.memset(s3w[:, 0:1, :], 0)
+        nc.vector.memset(s1w[:, 1:E, :], 0)
+        nc.vector.memset(s3w[:, 1:E, :], 0)
+        nc.vector.memset(s2w, 0)
+        ident = keep.tile([P, P], F32, name="ident")
+        def load_scales(queue, tile_words, source, e0, e1):
+            words = source.bitcast(I32)
+            for r in range(4):
+                queue.dma_start(tile_words[r:P:32, e0:e1, :], words[e0:e1, 0, r:16:4, :].rearrange("e q i -> q e i"))
+
+        def load_words(name, source):
+            tile = keep.tile([P, 2 * H], U8, name=name, align_bytes=64)
+            nc.sync.dma_start(tile[:].bitcast(I32), source.bitcast(I32))
+            return tile
+
+        w1, w3 = [], []
+        load_scales(nc.sync, s1w, w1_scales, 0, 1)
+        load_scales(nc.gpsimd, s3w, w3_scales, 0, 1)
+        make_identity(nc, ident[:])
+        w1.append(load_words("w1_0", w1_words[0, 0]))
+        w3.append(load_words("w3_0", w3_words[0, 0]))
+        w1.append(load_words("w1_1", w1_words[1, 0]))
+        w3.append(load_words("w3_1", w3_words[1, 0]))
+        load_scales(nc.sync, s1w, w1_scales, 1, E)
+        w2 = keep.tile([P, E * PASSES, 2 * N], U8, name="w2", align_bytes=64)
+        nc.sync.dma_start(w2[:].bitcast(I32), w2_words.bitcast(I32).rearrange("e s p c -> p (e s) c"))
+        for r in range(4):
+            nc.gpsimd.dma_start(
+                s2w[r:P:32, :, :], w2_scales.bitcast(I32)[:, :, r:16:4, :].rearrange("e s q i -> q (e s) i")
+            )
+        load_scales(nc.gpsimd, s3w, w3_scales, 1, E)
+        places = keep.tile([P, E * C // 16], U16, name="places")
+        nc.sync.dma_start(places[:], dst)
+        gates = keep.tile([P, E * C], F32, name="gates")
+        nc.sync.dma_start(gates[:], gate)
+        for e in range(2, E):
+            w1.append(load_words("w1_%d" % e, w1_words[e, 0]))
+            w3.append(load_words("w3_%d" % e, w3_words[e, 0]))
+
+        result = keep.tile([P, T], F32, name="result")
+        nc.gpsimd.memset(result[:], 0.0)
+
+        picked = keep.tile([P, 4, E * C], F32, name="picked")
+        for t in range(3):
+            nc.vector.tensor_copy(picked[:, t, :], planes[t][:].indirect(offsets[:]))
+
+        xq, xs = [], []
+        for e in range(E):
+            cols = slice(e * C, (e + 1) * C)
+            nc.vector.tensor_copy(picked[:, 3, cols], planes[3][:].indirect(offsets[:, e * C // 16 : (e + 1) * C // 16]))
+            xb = keep.tile([P, C, 4], BF16, name="xb%d" % e, align_bytes=64)
+            src = picked[:, :, cols].rearrange("p t (c i) -> p c t i", i=4)
+            dstv = xb[:].rearrange("p (c i) t -> p c t i", i=4)
+            if e == 0:
+                nc.vector.tensor_copy(dstv, src)
+            else:
+                nc.scalar.copy(dstv, src)
+            codes = keep.tile([P, C], U32, name="xq%d" % e, align_bytes=64)
+            scales = keep.tile([P, C], U8, name="xs%d" % e, align_bytes=64)
+            nc.vector.quantize_mx(out=codes[:].bitcast(FP8X4), scales=scales[:], in_=xb[:].rearrange("p n t -> p (n t)"))
+            xq.append(codes)
+            xs.append(scales)
+
+        units = [(e, g) for e in range(E) for g in range(PASSES)]
+        h_tiles = {}
+        t_tiles = {}
+        y_tiles = {}
+
+        def first_layer(u):
+            e, g = units[u]
+            cols = slice(g * HALF, (g + 1) * HALF)
+            a = psum_ab.tile([P, HALF], F32, name="a")
+            b = psum_ab.tile([P, HALF], F32, name="b")
+            for bank, w, s in ((a, w1[e], s1), (b, w3[e], s3)):
+                nc.tensor.matmul_mx(
+                    out=bank[:],
+                    lhsT=xq[e][:].bitcast(FP8X4),
+                    lhsT_scale=xs[e][:],
+                    rhs=w[:, 2 * g * HALF : 2 * (g + 1) * HALF].bitcast(FP4X4),
+                    rhs_scale=s[:, e, cols],
+                    start=True,
+                    stop=True,
+                )
+            ra = work.tile([P, HALF], F32, name="ra")
+            nc.scalar.activation(
+                ra[:].rearrange("s (u p d) -> s u p d", u=2, d=2), a[:].rearrange("s (p u d) -> s u p d", u=2, d=2), RELU
+            )
+            h = work.tile([P, HALF], BF16, name="h")
+            nc.vector.tensor_tensor(
+                h[:].rearrange("s (u p d) -> s u p d", u=2, d=2),
+                b[:].rearrange("s (p u d) -> s u p d", u=2, d=2),
+                ra[:].rearrange("s (u p d) -> s u p d", u=2, d=2),
+                MULT,
+            )
+            h_tiles[u] = h
+
+        def turn(u):
+            hw = h_tiles[u][:].bitcast(F32)
+            tp = psum_t.tile([P, 2, P], F32, name="tp")
+            for half in range(2):
+                nc.tensor.transpose(tp[:, half, :], hw[:, half * P : (half + 1) * P], ident[:])
+            ht = work.tile([P, C, 4], BF16, name="ht", align_bytes=64)
+            nc.scalar.copy(
+                ht[:].rearrange("p n t -> p (n t)").bitcast(F32).rearrange("p (n u) -> p n u", u=2),
+                tp[:].rearrange("p u n -> p n u"),
+            )
+            t_tiles[u] = ht
+
+        def second_layer(u):
+            e, g = units[u]
+            ht = t_tiles[u]
+            hq = work.tile([P, C], U32, name="hq", align_bytes=64)
+            hs = work.tile([P, C], U8, name="hs", align_bytes=64)
+            nc.vector.quantize_mx(out=hq[:].bitcast(FP8X4), scales=hs[:], in_=ht[:].rearrange("p n t -> p (n t)"))
+            if g == 0:
+                y_tiles[e] = psum_y.tile([P, C], F32, name="y")
+            y = y_tiles[e]
+            nc.tensor.matmul_mx(
+                out=y[:],
+                lhsT=w2[:, e * PASSES + g, :].bitcast(FP4X4),
+                lhsT_scale=s2[:, e * PASSES + g, :],
+                rhs=hq[:].bitcast(FP8X4),
+                rhs_scale=hs[:],
+                start=(g == 0),
+                stop=(g == PASSES - 1),
+            )
+            if g == PASSES - 1:
+                ys = work.tile([P, C], F32, name="ys")
+                nc.scalar.copy(ys[:], y[:])
+                nc.vector.tensor_tensor(
+                    result[:].indirect(places[:, e * C // 16 : (e + 1) * C // 16]),
+                    ys[:],
+                    gates[:, e * C : (e + 1) * C],
+                    MULT,
+                )
+
+        for step in range(len(units) + 2):
+            if step < len(units):
+                first_layer(step)
+            if 1 <= step <= len(units):
+                turn(step - 1)
+            if step >= 2:
+                second_layer(step - 2)
+        nc.sync.dma_start(out, result[:])

@@ -20,172 +20,208 @@ RELU = mybir.ActivationFunctionType.Relu
 
 HALF = 512
 PASSES = H // HALF
+SCALE_GROUPS = ((0, 4),)
 
 
 def tile_moe_two_glu_relu_kernel(tc, xT, w1_words, w1_scales, w3_words, w3_scales, w2_words, w2_scales, gate, offs, dst, out):
     nc = tc.nc
     with ExitStack() as ctx:
         keep = ctx.enter_context(tc.tile_pool(name="keep", bufs=1))
-        work = ctx.enter_context(tc.tile_pool(name="work", bufs=3))
+        work = ctx.enter_context(tc.tile_pool(name="work", bufs=4))
         psum_ab = ctx.enter_context(tc.psum_pool(name="psum_ab", bufs=2))
         psum_t = ctx.enter_context(tc.psum_pool(name="psum_t", bufs=2))
         psum_y = ctx.enter_context(tc.psum_pool(name="psum_y", bufs=2))
 
         offsets = keep.tile([P, E * C // 16], U16, name="offsets")
-        nc.sync.dma_start(offsets[:], offs)
-        xv = xT.rearrange("(p t) n -> p t n", t=4)
-        planes = []
-        for t in range(4):
-            plane = keep.tile([P, T], F32, name="plane%d" % t)
-            nc.sync.dma_start(plane[:], xv[:, t, :])
-            planes.append(plane)
-
-        s1 = keep.tile([P, E, H], U8, name="s1", align_bytes=64)
-        s3 = keep.tile([P, E, H], U8, name="s3", align_bytes=64)
-        s2 = keep.tile([P, E * PASSES, N], U8, name="s2", align_bytes=64)
-        s1w, s3w, s2w = s1[:].bitcast(I32), s3[:].bitcast(I32), s2[:].bitcast(I32)
-        nc.vector.memset(s1w[:, 0:1, :], 0)
-        nc.vector.memset(s3w[:, 0:1, :], 0)
-        nc.vector.memset(s1w[:, 1:E, :], 0)
-        nc.vector.memset(s3w[:, 1:E, :], 0)
-        nc.vector.memset(s2w, 0)
-        ident = keep.tile([P, P], F32, name="ident")
-        def load_scales(queue, tile_words, source, e0, e1):
-            words = source.bitcast(I32)
-            for r in range(4):
-                queue.dma_start(tile_words[r:P:32, e0:e1, :], words[e0:e1, 0, r:16:4, :].rearrange("e q i -> q e i"))
-
-        def load_words(name, source):
-            tile = keep.tile([P, 2 * H], U8, name=name, align_bytes=64)
-            nc.sync.dma_start(tile[:].bitcast(I32), source.bitcast(I32))
-            return tile
-
-        w1, w3 = [], []
-        load_scales(nc.sync, s1w, w1_scales, 0, 1)
-        load_scales(nc.gpsimd, s3w, w3_scales, 0, 1)
-        make_identity(nc, ident[:])
-        w1.append(load_words("w1_0", w1_words[0, 0]))
-        w3.append(load_words("w3_0", w3_words[0, 0]))
-        w1.append(load_words("w1_1", w1_words[1, 0]))
-        w3.append(load_words("w3_1", w3_words[1, 0]))
-        load_scales(nc.sync, s1w, w1_scales, 1, E)
-        w2 = keep.tile([P, E * PASSES, 2 * N], U8, name="w2", align_bytes=64)
-        nc.sync.dma_start(w2[:].bitcast(I32), w2_words.bitcast(I32).rearrange("e s p c -> p (e s) c"))
-        for r in range(4):
-            nc.gpsimd.dma_start(
-                s2w[r:P:32, :, :], w2_scales.bitcast(I32)[:, :, r:16:4, :].rearrange("e s q i -> q (e s) i")
-            )
-        load_scales(nc.gpsimd, s3w, w3_scales, 1, E)
         places = keep.tile([P, E * C // 16], U16, name="places")
-        nc.sync.dma_start(places[:], dst)
+        planes = [keep.tile([P, T], F32, name="plane%d" % t) for t in range(4)]
         gates = keep.tile([P, E * C], F32, name="gates")
-        nc.sync.dma_start(gates[:], gate)
-        for e in range(2, E):
-            w1.append(load_words("w1_%d" % e, w1_words[e, 0]))
-            w3.append(load_words("w3_%d" % e, w3_words[e, 0]))
-
+        w1 = [keep.tile([P, 2 * H], U8, name="w1_%d" % e, align_bytes=64) for e in range(E)]
+        w3 = [keep.tile([P, 2 * H], U8, name="w3_%d" % e, align_bytes=64) for e in range(E)]
+        w2 = keep.tile([P, E * PASSES, 2 * N], U8, name="w2", align_bytes=64)
+        s1 = [keep.tile([P, e1 - e0, H], U8, name="s1_%d" % e0, align_bytes=64) for e0, e1 in SCALE_GROUPS]
+        s3 = [keep.tile([P, e1 - e0, H], U8, name="s3_%d" % e0, align_bytes=64) for e0, e1 in SCALE_GROUPS]
+        s2 = keep.tile([P, E * PASSES, N], U8, name="s2", align_bytes=64)
+        ident = keep.tile([P, P], F32, name="ident")
         result = keep.tile([P, T], F32, name="result")
+
+        warm = keep.tile([P, 1], F32, name="warm")
+        nc.gpsimd.memset(warm[:], 0.0)
+        nc.scalar.activation(warm[:], warm[:], RELU)
+        for s in [tile for pair in zip(s1, s3) for tile in pair] + [s2]:
+            nc.vector.memset(s[:].bitcast(I32), 0)
+        make_identity(nc, ident[:])
         nc.gpsimd.memset(result[:], 0.0)
 
-        picked = keep.tile([P, 4, E * C], F32, name="picked")
-        for t in range(3):
-            nc.vector.tensor_copy(picked[:, t, :], planes[t][:].indirect(offsets[:]))
+        xv = xT.rearrange("(p t) n -> p t n", t=4)
 
-        xq, xs = [], []
-        for e in range(E):
-            cols = slice(e * C, (e + 1) * C)
-            nc.vector.tensor_copy(picked[:, 3, cols], planes[3][:].indirect(offsets[:, e * C // 16 : (e + 1) * C // 16]))
-            xb = keep.tile([P, C, 4], BF16, name="xb%d" % e, align_bytes=64)
-            src = picked[:, :, cols].rearrange("p t (c i) -> p c t i", i=4)
-            dstv = xb[:].rearrange("p (c i) t -> p c t i", i=4)
-            if e == 0:
-                nc.vector.tensor_copy(dstv, src)
-            else:
-                nc.scalar.copy(dstv, src)
-            codes = keep.tile([P, C], U32, name="xq%d" % e, align_bytes=64)
-            scales = keep.tile([P, C], U8, name="xs%d" % e, align_bytes=64)
-            nc.vector.quantize_mx(out=codes[:].bitcast(FP8X4), scales=scales[:], in_=xb[:].rearrange("p n t -> p (n t)"))
-            xq.append(codes)
-            xs.append(scales)
+        def load_scales(queue, tiles, source, group):
+            e0, e1 = SCALE_GROUPS[group]
+            words = source.bitcast(I32)
+            for r in range(4):
+                queue.dma_start(
+                    tiles[group][:].bitcast(I32)[r:P:32, :, :], words[e0:e1, 0, r:16:4, :].rearrange("e q i -> q e i")
+                )
+
+        def load_words(tiles, source, e):
+            nc.sync.dma_start(tiles[e][:].bitcast(I32), source[e, 0].bitcast(I32))
+
+        nc.sync.dma_start(planes[0][:], xv[:, 0, :])
+        nc.sync.dma_start(offsets[:], offs)
+        nc.sync.dma_start(planes[1][:], xv[:, 1, :])
+        nc.sync.dma_start(planes[2][:], xv[:, 2, :])
+        nc.sync.dma_start(planes[3][:], xv[:, 3, :])
+        load_scales(nc.sync, s1, w1_scales, 0)
+        load_words(w1, w1_words, 0)
+        load_scales(nc.sync, s3, w3_scales, 0)
+        load_words(w3, w3_words, 0)
+        load_words(w1, w1_words, 1)
+        load_words(w3, w3_words, 1)
+        for r in range(4):
+            nc.gpsimd.dma_start(
+                s2[:].bitcast(I32)[r:P:32, :, :], w2_scales.bitcast(I32)[:, :, r:16:4, :].rearrange("e s q i -> q (e s) i")
+            )
+        nc.sync.dma_start(w2[:].bitcast(I32), w2_words.bitcast(I32).rearrange("e s p c -> p (e s) c"))
+        load_words(w1, w1_words, 2)
+        load_words(w3, w3_words, 2)
+        nc.sync.dma_start(places[:], dst)
+        load_words(w1, w1_words, 3)
+        load_words(w3, w3_words, 3)
+        nc.sync.dma_start(gates[:], gate)
+
+        picked_first = keep.tile([P, 4, C], F32, name="picked_first")
+        picked_rest = keep.tile([P, 4, (E - 1) * C], F32, name="picked_rest")
+        xb = [keep.tile([P, C, 4], BF16, name="xb%d" % e, align_bytes=64) for e in range(E)]
+        xq = [keep.tile([P, C], U32, name="xq%d" % e, align_bytes=64) for e in range(E)]
+        xs = [keep.tile([P, C], U8, name="xs%d" % e, align_bytes=64) for e in range(E)]
+
+        def pick_first(t):
+            nc.vector.tensor_copy(picked_first[:, t, :], planes[t][:].indirect(offsets[:, 0 : C // 16]))
+
+        def pick_first_rounded(t):
+            nc.vector.tensor_copy(xb[0][:, :, t], planes[t][:].indirect(offsets[:, 0 : C // 16]))
+
+        def pick_rest(t):
+            nc.vector.tensor_copy(picked_rest[:, t, :], planes[t][:].indirect(offsets[:, C // 16 : E * C // 16]))
+
+        def interleave(e):
+            src = picked_rest[:, :, (e - 1) * C : e * C].rearrange("p t n -> p n t")
+            nc.gpsimd.tensor_copy(xb[e][:], src)
+
+        def quantise_tokens(e):
+            nc.vector.quantize_mx(
+                out=xq[e][:].bitcast(FP8X4), scales=xs[e][:], in_=xb[e][:].rearrange("p n t -> p (n t)")
+            )
+
+        for t in range(2):
+            pick_first(t)
+            pick_rest(t)
+        nc.scalar.copy(xb[0][:, :, 0:2], picked_first[:, 0:2, :].rearrange("p t n -> p n t"))
+        pick_first_rounded(2)
+        pick_rest(2)
+        pick_first_rounded(3)
+        quantise_tokens(0)
+        pick_rest(3)
+        for e in range(1, E):
+            interleave(e)
 
         units = [(e, g) for e in range(E) for g in range(PASSES)]
-        h_tiles = {}
-        t_tiles = {}
-        y_tiles = {}
+        a_banks, b_banks, relus, h_tiles, tp_tiles, t_tiles, hq_tiles, y_tiles, ys_tiles = {}, {}, {}, {}, {}, {}, {}, {}, {}
 
-        def first_layer(u):
+        def scales_of(tiles, e):
+            for tile, (e0, e1) in zip(tiles, SCALE_GROUPS):
+                if e0 <= e < e1:
+                    return tile[:, e - e0, :]
+
+        def multiply_first(u, banks, name, words, scales):
             e, g = units[u]
-            cols = slice(g * HALF, (g + 1) * HALF)
-            a = psum_ab.tile([P, HALF], F32, name="a")
-            b = psum_ab.tile([P, HALF], F32, name="b")
-            for bank, w, s in ((a, w1[e], s1), (b, w3[e], s3)):
-                nc.tensor.matmul_mx(
-                    out=bank[:],
-                    lhsT=xq[e][:].bitcast(FP8X4),
-                    lhsT_scale=xs[e][:],
-                    rhs=w[:, 2 * g * HALF : 2 * (g + 1) * HALF].bitcast(FP4X4),
-                    rhs_scale=s[:, e, cols],
-                    start=True,
-                    stop=True,
-                )
-            ra = work.tile([P, HALF], F32, name="ra")
-            nc.scalar.activation(
-                ra[:].rearrange("s (u p d) -> s u p d", u=2, d=2), a[:].rearrange("s (p u d) -> s u p d", u=2, d=2), RELU
+            banks[u] = psum_ab.tile([P, HALF], F32, name=name)
+            nc.tensor.matmul_mx(
+                out=banks[u][:],
+                lhsT=xq[e][:].bitcast(FP8X4),
+                lhsT_scale=xs[e][:],
+                rhs=words[e][:, 2 * g * HALF : 2 * (g + 1) * HALF].bitcast(FP4X4),
+                rhs_scale=scales_of(scales, e)[:, g * HALF : (g + 1) * HALF],
+                start=True,
+                stop=True,
             )
-            h = work.tile([P, HALF], BF16, name="h")
+
+        def multiply_a(u):
+            multiply_first(u, a_banks, "a", w1, s1)
+
+        def multiply_b(u):
+            multiply_first(u, b_banks, "b", w3, s3)
+
+        def rectify(u):
+            relus[u] = work.tile([P, HALF], F32, name="ra")
+            nc.scalar.activation(
+                relus[u][:].rearrange("s (u p d) -> s u p d", u=2, d=2),
+                a_banks[u][:].rearrange("s (p u d) -> s u p d", u=2, d=2),
+                RELU,
+            )
+
+        def gate_hidden(u):
+            h_tiles[u] = work.tile([P, HALF], BF16, name="h")
             nc.vector.tensor_tensor(
-                h[:].rearrange("s (u p d) -> s u p d", u=2, d=2),
-                b[:].rearrange("s (p u d) -> s u p d", u=2, d=2),
-                ra[:].rearrange("s (u p d) -> s u p d", u=2, d=2),
+                h_tiles[u][:].rearrange("s (u p d) -> s u p d", u=2, d=2),
+                b_banks[u][:].rearrange("s (p u d) -> s u p d", u=2, d=2),
+                relus[u][:].rearrange("s (u p d) -> s u p d", u=2, d=2),
                 MULT,
             )
-            h_tiles[u] = h
 
         def turn(u):
             hw = h_tiles[u][:].bitcast(F32)
-            tp = psum_t.tile([P, 2, P], F32, name="tp")
+            tp_tiles[u] = psum_t.tile([P, 2, P], F32, name="tp")
             for half in range(2):
-                nc.tensor.transpose(tp[:, half, :], hw[:, half * P : (half + 1) * P], ident[:])
-            ht = work.tile([P, C, 4], BF16, name="ht", align_bytes=64)
-            nc.scalar.copy(
-                ht[:].rearrange("p n t -> p (n t)").bitcast(F32).rearrange("p (n u) -> p n u", u=2),
-                tp[:].rearrange("p u n -> p n u"),
-            )
-            t_tiles[u] = ht
+                nc.tensor.transpose(tp_tiles[u][:, half, :], hw[:, half * P : (half + 1) * P], ident[:])
 
-        def second_layer(u):
+        def empty_turned(u):
+            t_tiles[u] = work.tile([P, C, 4], BF16, name="ht", align_bytes=64)
+            nc.scalar.copy(
+                t_tiles[u][:].rearrange("p n t -> p (n t)").bitcast(F32).rearrange("p (n u) -> p n u", u=2),
+                tp_tiles[u][:].rearrange("p u n -> p n u"),
+            )
+
+        def quantise_hidden(u):
+            codes = work.tile([P, C], U32, name="hq", align_bytes=64)
+            scales = work.tile([P, C], U8, name="hs", align_bytes=64)
+            nc.vector.quantize_mx(
+                out=codes[:].bitcast(FP8X4), scales=scales[:], in_=t_tiles[u][:].rearrange("p n t -> p (n t)")
+            )
+            hq_tiles[u] = (codes, scales)
+
+        def multiply_second(u):
             e, g = units[u]
-            ht = t_tiles[u]
-            hq = work.tile([P, C], U32, name="hq", align_bytes=64)
-            hs = work.tile([P, C], U8, name="hs", align_bytes=64)
-            nc.vector.quantize_mx(out=hq[:].bitcast(FP8X4), scales=hs[:], in_=ht[:].rearrange("p n t -> p (n t)"))
             if g == 0:
                 y_tiles[e] = psum_y.tile([P, C], F32, name="y")
-            y = y_tiles[e]
             nc.tensor.matmul_mx(
-                out=y[:],
+                out=y_tiles[e][:],
                 lhsT=w2[:, e * PASSES + g, :].bitcast(FP4X4),
                 lhsT_scale=s2[:, e * PASSES + g, :],
-                rhs=hq[:].bitcast(FP8X4),
-                rhs_scale=hs[:],
+                rhs=hq_tiles[u][0][:].bitcast(FP8X4),
+                rhs_scale=hq_tiles[u][1][:],
                 start=(g == 0),
                 stop=(g == PASSES - 1),
             )
-            if g == PASSES - 1:
-                ys = work.tile([P, C], F32, name="ys")
-                nc.scalar.copy(ys[:], y[:])
-                nc.vector.tensor_tensor(
-                    result[:].indirect(places[:, e * C // 16 : (e + 1) * C // 16]),
-                    ys[:],
-                    gates[:, e * C : (e + 1) * C],
-                    MULT,
-                )
 
-        for step in range(len(units) + 2):
-            if step < len(units):
-                first_layer(step)
-            if 1 <= step <= len(units):
-                turn(step - 1)
-            if step >= 2:
-                second_layer(step - 2)
+        def take_out(e):
+            ys_tiles[e] = work.tile([P, C], F32, name="ys")
+            nc.scalar.copy(ys_tiles[e][:], y_tiles[e][:])
+
+        def send_back(e):
+            nc.vector.tensor_tensor(
+                result[:].indirect(places[:, e * C // 16 : (e + 1) * C // 16]),
+                ys_tiles[e][:],
+                gates[:, e * C : (e + 1) * C],
+                MULT,
+            )
+
+        calls = {
+            "a": multiply_a, "b": multiply_b, "r": rectify, "m": gate_hidden, "t": turn, "c": empty_turned,
+            "q": quantise_hidden, "s": multiply_second, "x": lambda u: quantise_tokens(u // 2),
+            "y": lambda u: take_out(u // 2), "z": lambda u: send_back(u // 2),
+        }
+        order = "a0 a1 b0 r0 x2 b1 m0 r1 x4 a2 a3 m1 t0 r2 b2 t1 m2 c0 x6 b3 a4 r3 c1 b4 a5 t2 q0 m3 q1 t3 r4 m4 b5 s0 r5 m5 a6 a7 b6 c3 c2 r6 q2 r7 t4 b7 q3 c4 t5 s1 m6 c5 m7 s2 y1 q4 t6 t7 c6 s3 s4 q5 c7 y3 s5 z1 q6 q7 s6 y5 s7 z3 y7 z5 z7"
+        for word in order.split(" "):
+            calls[word[0:1]](int(word[1:2]))
         nc.sync.dma_start(out, result[:])

@@ -17,70 +17,69 @@ FP8X4 = mybir.dt.float8_e4m3fn_x4
 FP4X4 = mybir.dt.float4_e2m1fn_x4
 MULT = mybir.AluOpType.mult
 RELU = mybir.ActivationFunctionType.Relu
+COPY = mybir.ActivationFunctionType.Copy
 
+PACK = 4
 HALF = 512
 PASSES = H // HALF
-SCALE_GROUPS = ((0, 4),)
+SCALE_ROWS = 16
+LIST_COLS = C // 16
 
 
-def tile_moe_two_glu_relu_kernel(tc, xT, w1_words, w1_scales, w3_words, w3_scales, w2_words, w2_scales, gate, offs, dst, out):
+def tile_moe_two_glu_relu_kernel(
+    tc, xT, w1_words, w1_scales, w3_words, w3_scales, w2_words, w2_scales, gate, offs, dst, out
+):
     nc = tc.nc
     with ExitStack() as ctx:
         keep = ctx.enter_context(tc.tile_pool(name="keep", bufs=1))
         work = ctx.enter_context(tc.tile_pool(name="work", bufs=4))
-        psum_ab = ctx.enter_context(tc.psum_pool(name="psum_ab", bufs=2))
-        psum_t = ctx.enter_context(tc.psum_pool(name="psum_t", bufs=2))
-        psum_y = ctx.enter_context(tc.psum_pool(name="psum_y", bufs=2))
+        psum_first = ctx.enter_context(tc.psum_pool(name="psum_first", bufs=2))
+        psum_turned = ctx.enter_context(tc.psum_pool(name="psum_turned", bufs=2))
+        psum_second = ctx.enter_context(tc.psum_pool(name="psum_second", bufs=2))
 
-        offsets = keep.tile([P, E * C // 16], U16, name="offsets")
-        places = keep.tile([P, E * C // 16], U16, name="places")
-        planes = [keep.tile([P, T], F32, name="plane%d" % t) for t in range(4)]
+        sources = keep.tile([P, E * LIST_COLS], U16, name="sources")
+        places = keep.tile([P, E * LIST_COLS], U16, name="places")
+        planes = [keep.tile([P, T], F32, name="plane%d" % t) for t in range(PACK)]
         gates = keep.tile([P, E * C], F32, name="gates")
         w1 = [keep.tile([P, 2 * H], U8, name="w1_%d" % e, align_bytes=64) for e in range(E)]
         w3 = [keep.tile([P, 2 * H], U8, name="w3_%d" % e, align_bytes=64) for e in range(E)]
         w2 = keep.tile([P, E * PASSES, 2 * N], U8, name="w2", align_bytes=64)
-        s1 = [keep.tile([P, e1 - e0, H], U8, name="s1_%d" % e0, align_bytes=64) for e0, e1 in SCALE_GROUPS]
-        s3 = [keep.tile([P, e1 - e0, H], U8, name="s3_%d" % e0, align_bytes=64) for e0, e1 in SCALE_GROUPS]
+        s1 = keep.tile([P, E, H], U8, name="s1", align_bytes=64)
+        s3 = keep.tile([P, E, H], U8, name="s3", align_bytes=64)
         s2 = keep.tile([P, E * PASSES, N], U8, name="s2", align_bytes=64)
-        ident = keep.tile([P, P], F32, name="ident")
+        identity = keep.tile([P, P], F32, name="identity")
         result = keep.tile([P, T], F32, name="result")
 
-        warm = keep.tile([P, 1], F32, name="warm")
-        nc.gpsimd.memset(warm[:], 0.0)
-        nc.scalar.activation(warm[:], warm[:], RELU)
-        for s in [tile for pair in zip(s1, s3) for tile in pair] + [s2]:
-            nc.vector.memset(s[:].bitcast(I32), 0)
-        make_identity(nc, ident[:])
+        column = keep.tile([P, 1], F32, name="column")
+        nc.gpsimd.memset(column[:], 0.0)
+        nc.scalar.activation(column[:], column[:], RELU)
+        for scales in (s1, s3, s2):
+            nc.vector.memset(scales[:].bitcast(I32), 0)
+        make_identity(nc, identity[:])
         nc.gpsimd.memset(result[:], 0.0)
 
-        xv = xT.rearrange("(p t) n -> p t n", t=4)
+        def load_plane(t):
+            nc.sync.dma_start(planes[t][:], xT.rearrange("(p t) n -> p t n", t=PACK)[:, t, :])
 
-        def load_scales(queue, tiles, source, group):
-            e0, e1 = SCALE_GROUPS[group]
-            words = source.bitcast(I32)
+        def load_words(tiles, words, e):
+            nc.sync.dma_start(tiles[e][:].bitcast(I32), words[e, 0].bitcast(I32))
+
+        def load_scales(queue, tile, rows):
             for r in range(4):
-                queue.dma_start(
-                    tiles[group][:].bitcast(I32)[r:P:32, :, :], words[e0:e1, 0, r:16:4, :].rearrange("e q i -> q e i")
-                )
+                queue.dma_start(tile[:].bitcast(I32)[r:P:32, :, :], rows[:, r:SCALE_ROWS:4, :].rearrange("m q c -> q m c"))
 
-        def load_words(tiles, source, e):
-            nc.sync.dma_start(tiles[e][:].bitcast(I32), source[e, 0].bitcast(I32))
-
-        nc.sync.dma_start(planes[0][:], xv[:, 0, :])
-        nc.sync.dma_start(offsets[:], offs)
-        nc.sync.dma_start(planes[1][:], xv[:, 1, :])
-        nc.sync.dma_start(planes[2][:], xv[:, 2, :])
-        nc.sync.dma_start(planes[3][:], xv[:, 3, :])
-        load_scales(nc.sync, s1, w1_scales, 0)
+        load_plane(0)
+        nc.sync.dma_start(sources[:], offs)
+        load_plane(1)
+        load_plane(2)
+        load_plane(3)
+        load_scales(nc.sync, s1, w1_scales.bitcast(I32).rearrange("e s q i -> (e s) q i"))
         load_words(w1, w1_words, 0)
-        load_scales(nc.sync, s3, w3_scales, 0)
+        load_scales(nc.sync, s3, w3_scales.bitcast(I32).rearrange("e s q i -> (e s) q i"))
         load_words(w3, w3_words, 0)
         load_words(w1, w1_words, 1)
         load_words(w3, w3_words, 1)
-        for r in range(4):
-            nc.gpsimd.dma_start(
-                s2[:].bitcast(I32)[r:P:32, :, :], w2_scales.bitcast(I32)[:, :, r:16:4, :].rearrange("e s q i -> q (e s) i")
-            )
+        load_scales(nc.gpsimd, s2, w2_scales.bitcast(I32).rearrange("e s q n -> (e s) q n"))
         nc.sync.dma_start(w2[:].bitcast(I32), w2_words.bitcast(I32).rearrange("e s p c -> p (e s) c"))
         load_words(w1, w1_words, 2)
         load_words(w3, w3_words, 2)
@@ -89,139 +88,141 @@ def tile_moe_two_glu_relu_kernel(tc, xT, w1_words, w1_scales, w3_words, w3_scale
         load_words(w3, w3_words, 3)
         nc.sync.dma_start(gates[:], gate)
 
-        picked_first = keep.tile([P, 4, C], F32, name="picked_first")
-        picked_rest = keep.tile([P, 4, (E - 1) * C], F32, name="picked_rest")
-        xb = [keep.tile([P, C, 4], BF16, name="xb%d" % e, align_bytes=64) for e in range(E)]
-        xq = [keep.tile([P, C], U32, name="xq%d" % e, align_bytes=64) for e in range(E)]
-        xs = [keep.tile([P, C], U8, name="xs%d" % e, align_bytes=64) for e in range(E)]
+        rounded = [keep.tile([P, T], BF16, name="rounded%d" % t, align_bytes=64) for t in range(2)]
+        tokens = [keep.tile([P, C, PACK], BF16, name="tokens%d" % e, align_bytes=64) for e in range(E)]
+        token_codes = [keep.tile([P, C], U32, name="token_codes%d" % e, align_bytes=64) for e in range(E)]
+        token_scales = [keep.tile([P, C], U8, name="token_scales%d" % e, align_bytes=64) for e in range(E)]
 
-        def pick_first(t):
-            nc.vector.tensor_copy(picked_first[:, t, :], planes[t][:].indirect(offsets[:, 0 : C // 16]))
+        def slots_of(offsets, e):
+            return offsets[:, e * LIST_COLS : (e + 1) * LIST_COLS]
 
-        def pick_first_rounded(t):
-            nc.vector.tensor_copy(xb[0][:, :, t], planes[t][:].indirect(offsets[:, 0 : C // 16]))
-
-        def pick_rest(t):
-            nc.vector.tensor_copy(picked_rest[:, t, :], planes[t][:].indirect(offsets[:, C // 16 : E * C // 16]))
-
-        def interleave(e):
-            src = picked_rest[:, :, (e - 1) * C : e * C].rearrange("p t n -> p n t")
-            nc.gpsimd.tensor_copy(xb[e][:], src)
+        def pick(e, t):
+            if t < 2:
+                nc.scalar.activation(tokens[e][:, :, t], rounded[t][:].indirect(slots_of(sources, e)), COPY)
+            else:
+                nc.vector.tensor_copy(tokens[e][:, :, t], planes[t][:].indirect(slots_of(sources, e)))
 
         def quantise_tokens(e):
             nc.vector.quantize_mx(
-                out=xq[e][:].bitcast(FP8X4), scales=xs[e][:], in_=xb[e][:].rearrange("p n t -> p (n t)")
+                out=token_codes[e][:].bitcast(FP8X4),
+                scales=token_scales[e][:],
+                in_=tokens[e][:].rearrange("p c t -> p (c t)"),
             )
 
         for t in range(2):
-            pick_first(t)
-            pick_rest(t)
-        nc.scalar.copy(xb[0][:, :, 0:2], picked_first[:, 0:2, :].rearrange("p t n -> p n t"))
-        pick_first_rounded(2)
-        pick_rest(2)
-        pick_first_rounded(3)
-        quantise_tokens(0)
-        pick_rest(3)
-        for e in range(1, E):
-            interleave(e)
+            nc.vector.tensor_copy(rounded[t][:], planes[t][:])
+        for e in range(E):
+            for t in range(PACK):
+                pick(e, t)
+            if e == 0:
+                quantise_tokens(e)
 
-        units = [(e, g) for e in range(E) for g in range(PASSES)]
-        a_banks, b_banks, relus, h_tiles, tp_tiles, t_tiles, hq_tiles, y_tiles, ys_tiles = {}, {}, {}, {}, {}, {}, {}, {}, {}
+        a_banks, b_banks, relus, hidden, turned_banks, turned, hidden_codes, hidden_scales = {}, {}, {}, {}, {}, {}, {}, {}
+        y_banks, y_copies = {}, {}
 
-        def scales_of(tiles, e):
-            for tile, (e0, e1) in zip(tiles, SCALE_GROUPS):
-                if e0 <= e < e1:
-                    return tile[:, e - e0, :]
-
-        def multiply_first(u, banks, name, words, scales):
-            e, g = units[u]
-            banks[u] = psum_ab.tile([P, HALF], F32, name=name)
+        def multiply_first(banks, name, words, scales, u):
+            e, g = u // PASSES, u % PASSES
+            banks[u] = psum_first.tile([P, HALF], F32, name=name)
             nc.tensor.matmul_mx(
                 out=banks[u][:],
-                lhsT=xq[e][:].bitcast(FP8X4),
-                lhsT_scale=xs[e][:],
+                lhsT=token_codes[e][:].bitcast(FP8X4),
+                lhsT_scale=token_scales[e][:],
                 rhs=words[e][:, 2 * g * HALF : 2 * (g + 1) * HALF].bitcast(FP4X4),
-                rhs_scale=scales_of(scales, e)[:, g * HALF : (g + 1) * HALF],
+                rhs_scale=scales[:, e, g * HALF : (g + 1) * HALF],
                 start=True,
                 stop=True,
             )
 
         def multiply_a(u):
-            multiply_first(u, a_banks, "a", w1, s1)
+            multiply_first(a_banks, "a", w1, s1, u)
 
         def multiply_b(u):
-            multiply_first(u, b_banks, "b", w3, s3)
+            multiply_first(b_banks, "b", w3, s3, u)
+
+        def bank_order(bank):
+            return bank[:].rearrange("s (m v d) -> s v m d", v=2, d=2)
+
+        def pair_order(tile):
+            return tile[:].rearrange("s (v m d) -> s v m d", v=2, d=2)
 
         def rectify(u):
-            relus[u] = work.tile([P, HALF], F32, name="ra")
-            nc.scalar.activation(
-                relus[u][:].rearrange("s (u p d) -> s u p d", u=2, d=2),
-                a_banks[u][:].rearrange("s (p u d) -> s u p d", u=2, d=2),
-                RELU,
-            )
+            relus[u] = work.tile([P, HALF], F32, name="relu")
+            nc.scalar.activation(pair_order(relus[u]), bank_order(a_banks[u]), RELU)
 
         def gate_hidden(u):
-            h_tiles[u] = work.tile([P, HALF], BF16, name="h")
-            nc.vector.tensor_tensor(
-                h_tiles[u][:].rearrange("s (u p d) -> s u p d", u=2, d=2),
-                b_banks[u][:].rearrange("s (p u d) -> s u p d", u=2, d=2),
-                relus[u][:].rearrange("s (u p d) -> s u p d", u=2, d=2),
-                MULT,
-            )
+            hidden[u] = work.tile([P, HALF], BF16, name="hidden")
+            nc.vector.tensor_tensor(pair_order(hidden[u]), bank_order(b_banks[u]), pair_order(relus[u]), MULT)
 
         def turn(u):
-            hw = h_tiles[u][:].bitcast(F32)
-            tp_tiles[u] = psum_t.tile([P, 2, P], F32, name="tp")
-            for half in range(2):
-                nc.tensor.transpose(tp_tiles[u][:, half, :], hw[:, half * P : (half + 1) * P], ident[:])
+            pairs = hidden[u][:].bitcast(F32)
+            turned_banks[u] = psum_turned.tile([P, 2, C], F32, name="turned_bank")
+            for v in range(2):
+                nc.tensor.transpose(turned_banks[u][:, v, :], pairs[:, v * P : (v + 1) * P], identity[:])
 
         def empty_turned(u):
-            t_tiles[u] = work.tile([P, C, 4], BF16, name="ht", align_bytes=64)
+            turned[u] = work.tile([P, C, PACK], BF16, name="turned", align_bytes=64)
             nc.scalar.copy(
-                t_tiles[u][:].rearrange("p n t -> p (n t)").bitcast(F32).rearrange("p (n u) -> p n u", u=2),
-                tp_tiles[u][:].rearrange("p u n -> p n u"),
+                turned[u][:].rearrange("p c t -> p (c t)").bitcast(F32).rearrange("p (c v) -> p c v", v=2),
+                turned_banks[u][:].rearrange("p v c -> p c v"),
             )
 
         def quantise_hidden(u):
-            codes = work.tile([P, C], U32, name="hq", align_bytes=64)
-            scales = work.tile([P, C], U8, name="hs", align_bytes=64)
+            hidden_codes[u] = work.tile([P, C], U32, name="hidden_codes", align_bytes=64)
+            hidden_scales[u] = work.tile([P, C], U8, name="hidden_scales", align_bytes=64)
             nc.vector.quantize_mx(
-                out=codes[:].bitcast(FP8X4), scales=scales[:], in_=t_tiles[u][:].rearrange("p n t -> p (n t)")
+                out=hidden_codes[u][:].bitcast(FP8X4),
+                scales=hidden_scales[u][:],
+                in_=turned[u][:].rearrange("p c t -> p (c t)"),
             )
-            hq_tiles[u] = (codes, scales)
 
         def multiply_second(u):
-            e, g = units[u]
+            e, g = u // PASSES, u % PASSES
             if g == 0:
-                y_tiles[e] = psum_y.tile([P, C], F32, name="y")
+                y_banks[e] = psum_second.tile([P, C], F32, name="y_bank")
             nc.tensor.matmul_mx(
-                out=y_tiles[e][:],
-                lhsT=w2[:, e * PASSES + g, :].bitcast(FP4X4),
-                lhsT_scale=s2[:, e * PASSES + g, :],
-                rhs=hq_tiles[u][0][:].bitcast(FP8X4),
-                rhs_scale=hq_tiles[u][1][:],
+                out=y_banks[e][:],
+                lhsT=w2[:, u, :].bitcast(FP4X4),
+                lhsT_scale=s2[:, u, :],
+                rhs=hidden_codes[u][:].bitcast(FP8X4),
+                rhs_scale=hidden_scales[u][:],
                 start=(g == 0),
                 stop=(g == PASSES - 1),
             )
 
         def take_out(e):
-            ys_tiles[e] = work.tile([P, C], F32, name="ys")
-            nc.scalar.copy(ys_tiles[e][:], y_tiles[e][:])
+            y_copies[e] = work.tile([P, C], F32, name="y_copy")
+            nc.scalar.copy(y_copies[e][:], y_banks[e][:])
 
         def send_back(e):
             nc.vector.tensor_tensor(
-                result[:].indirect(places[:, e * C // 16 : (e + 1) * C // 16]),
-                ys_tiles[e][:],
-                gates[:, e * C : (e + 1) * C],
-                MULT,
+                result[:].indirect(slots_of(places, e)), y_copies[e][:], gates[:, e * C : (e + 1) * C], MULT
             )
 
-        calls = {
-            "a": multiply_a, "b": multiply_b, "r": rectify, "m": gate_hidden, "t": turn, "c": empty_turned,
-            "q": quantise_hidden, "s": multiply_second, "x": lambda u: quantise_tokens(u // 2),
-            "y": lambda u: take_out(u // 2), "z": lambda u: send_back(u // 2),
-        }
-        order = "a0 a1 b0 r0 x2 b1 m0 r1 x4 a2 a3 m1 t0 r2 b2 t1 m2 c0 x6 b3 a4 r3 c1 b4 a5 t2 q0 m3 q1 t3 r4 m4 b5 s0 r5 m5 a6 a7 b6 c3 c2 r6 q2 r7 t4 b7 q3 c4 t5 s1 m6 c5 m7 s2 y1 q4 t6 t7 c6 s3 s4 q5 c7 y3 s5 z1 q6 q7 s6 y5 s7 z3 y7 z5 z7"
-        for word in order.split(" "):
-            calls[word[0:1]](int(word[1:2]))
+        calls = (
+            (multiply_a, 0, 0),
+            (multiply_a, 0, 1),
+            (rectify, 0, 0),
+            (quantise_hidden, 2, 0),
+            (multiply_b, 0, 0),
+            (quantise_hidden, 2, 1),
+            (take_out, 4, None),
+            (turn, 1, 0),
+            (turn, 1, 1),
+            (multiply_b, 0, 1),
+            (rectify, 0, 1),
+            (empty_turned, 1, 0),
+            (gate_hidden, 0, 0),
+            (quantise_tokens, -1, None),
+            (empty_turned, 1, 1),
+            (multiply_second, 3, 1),
+            (multiply_second, 2, 0),
+            (gate_hidden, 0, 1),
+            (send_back, 4, None),
+        )
+        longest_lag = max(lag for call, lag, g in calls)
+        for step in range(E + longest_lag):
+            for call, lag, g in calls:
+                e = step - lag
+                if 0 <= e < E and (call is not quantise_tokens or e > 0):
+                    call(e if g is None else e * PASSES + g)
         nc.sync.dma_start(out, result[:])

from contextlib import ExitStack

import concourse.mybir as mybir
from concourse.masks import make_identity

K, T, E, C, H, N = 512, 1024, 4, 128, 1024, 128
P = 128
FLOPS = 2 * E * C * (2 * K * H + H * N)

F32 = mybir.dt.float32
BF16 = mybir.dt.bfloat16
I32 = mybir.dt.int32
U32 = mybir.dt.uint32
U16 = mybir.dt.uint16
U8 = mybir.dt.uint8
FP8X4 = mybir.dt.float8_e4m3fn_x4
FP4X4 = mybir.dt.float4_e2m1fn_x4
MULT = mybir.AluOpType.mult
RELU = mybir.ActivationFunctionType.Relu
COPY = mybir.ActivationFunctionType.Copy

PACK = 4
HALF = 512
PASSES = H // HALF
SCALE_ROWS = 16
LIST_COLS = C // 16


def tile_moe_two_glu_relu_kernel(
    tc, xT, w1_words, w1_scales, w3_words, w3_scales, w2_words, w2_scales, gate, offs, dst, out
):
    nc = tc.nc
    with ExitStack() as ctx:
        keep = ctx.enter_context(tc.tile_pool(name="keep", bufs=1))
        work = ctx.enter_context(tc.tile_pool(name="work", bufs=4))
        psum_first = ctx.enter_context(tc.psum_pool(name="psum_first", bufs=2))
        psum_turned = ctx.enter_context(tc.psum_pool(name="psum_turned", bufs=2))
        psum_second = ctx.enter_context(tc.psum_pool(name="psum_second", bufs=2))

        sources = keep.tile([P, E * LIST_COLS], U16, name="sources")
        places = keep.tile([P, E * LIST_COLS], U16, name="places")
        planes = [keep.tile([P, T], F32, name="plane%d" % t) for t in range(PACK)]
        gates = keep.tile([P, E * C], F32, name="gates")
        w1 = [keep.tile([P, 2 * H], U8, name="w1_%d" % e, align_bytes=64) for e in range(E)]
        w3 = [keep.tile([P, 2 * H], U8, name="w3_%d" % e, align_bytes=64) for e in range(E)]
        w2 = keep.tile([P, E * PASSES, 2 * N], U8, name="w2", align_bytes=64)
        s1 = keep.tile([P, E, H], U8, name="s1", align_bytes=64)
        s3 = keep.tile([P, E, H], U8, name="s3", align_bytes=64)
        s2 = keep.tile([P, E * PASSES, N], U8, name="s2", align_bytes=64)
        identity = keep.tile([P, P], F32, name="identity")
        result = keep.tile([P, T], F32, name="result")

        column = keep.tile([P, 1], F32, name="column")
        nc.gpsimd.memset(column[:], 0.0)
        nc.scalar.activation(column[:], column[:], RELU)
        for scales in (s1, s3, s2):
            nc.vector.memset(scales[:].bitcast(I32), 0)
        make_identity(nc, identity[:])
        nc.gpsimd.memset(result[:], 0.0)

        def load_plane(t):
            nc.sync.dma_start(planes[t][:], xT.rearrange("(p t) n -> p t n", t=PACK)[:, t, :])

        def load_words(tiles, words, e):
            nc.sync.dma_start(tiles[e][:].bitcast(I32), words[e, 0].bitcast(I32))

        def load_scales(queue, tile, rows):
            for r in range(4):
                queue.dma_start(tile[:].bitcast(I32)[r:P:32, :, :], rows[:, r:SCALE_ROWS:4, :].rearrange("m q c -> q m c"))

        load_plane(0)
        nc.sync.dma_start(sources[:], offs)
        load_plane(1)
        load_plane(2)
        load_plane(3)
        load_scales(nc.sync, s1, w1_scales.bitcast(I32).rearrange("e s q i -> (e s) q i"))
        load_words(w1, w1_words, 0)
        load_scales(nc.sync, s3, w3_scales.bitcast(I32).rearrange("e s q i -> (e s) q i"))
        load_words(w3, w3_words, 0)
        load_words(w1, w1_words, 1)
        load_words(w3, w3_words, 1)
        load_scales(nc.gpsimd, s2, w2_scales.bitcast(I32).rearrange("e s q n -> (e s) q n"))
        nc.sync.dma_start(w2[:].bitcast(I32), w2_words.bitcast(I32).rearrange("e s p c -> p (e s) c"))
        load_words(w1, w1_words, 2)
        load_words(w3, w3_words, 2)
        nc.sync.dma_start(places[:], dst)
        load_words(w1, w1_words, 3)
        load_words(w3, w3_words, 3)
        nc.sync.dma_start(gates[:], gate)

        rounded = [keep.tile([P, T], BF16, name="rounded%d" % t, align_bytes=64) for t in range(2)]
        tokens = [keep.tile([P, C, PACK], BF16, name="tokens%d" % e, align_bytes=64) for e in range(E)]
        token_codes = [keep.tile([P, C], U32, name="token_codes%d" % e, align_bytes=64) for e in range(E)]
        token_scales = [keep.tile([P, C], U8, name="token_scales%d" % e, align_bytes=64) for e in range(E)]

        def slots_of(offsets, e):
            return offsets[:, e * LIST_COLS : (e + 1) * LIST_COLS]

        def pick(e, t):
            if t < 2:
                nc.scalar.activation(tokens[e][:, :, t], rounded[t][:].indirect(slots_of(sources, e)), COPY)
            else:
                nc.vector.tensor_copy(tokens[e][:, :, t], planes[t][:].indirect(slots_of(sources, e)))

        def quantise_tokens(e):
            nc.vector.quantize_mx(
                out=token_codes[e][:].bitcast(FP8X4),
                scales=token_scales[e][:],
                in_=tokens[e][:].rearrange("p c t -> p (c t)"),
            )

        for t in range(2):
            nc.vector.tensor_copy(rounded[t][:], planes[t][:])
        for e in range(E):
            for t in range(PACK):
                pick(e, t)
            if e == 0:
                quantise_tokens(e)

        a_banks, b_banks, relus, hidden, turned_banks, turned, hidden_codes, hidden_scales = {}, {}, {}, {}, {}, {}, {}, {}
        y_banks, y_copies = {}, {}

        def multiply_first(banks, name, words, scales, u):
            e, g = u // PASSES, u % PASSES
            banks[u] = psum_first.tile([P, HALF], F32, name=name)
            nc.tensor.matmul_mx(
                out=banks[u][:],
                lhsT=token_codes[e][:].bitcast(FP8X4),
                lhsT_scale=token_scales[e][:],
                rhs=words[e][:, 2 * g * HALF : 2 * (g + 1) * HALF].bitcast(FP4X4),
                rhs_scale=scales[:, e, g * HALF : (g + 1) * HALF],
                start=True,
                stop=True,
            )

        def multiply_a(u):
            multiply_first(a_banks, "a", w1, s1, u)

        def multiply_b(u):
            multiply_first(b_banks, "b", w3, s3, u)

        def bank_order(bank):
            return bank[:].rearrange("s (m v d) -> s v m d", v=2, d=2)

        def pair_order(tile):
            return tile[:].rearrange("s (v m d) -> s v m d", v=2, d=2)

        def rectify(u):
            relus[u] = work.tile([P, HALF], F32, name="relu")
            nc.scalar.activation(pair_order(relus[u]), bank_order(a_banks[u]), RELU)

        def gate_hidden(u):
            hidden[u] = work.tile([P, HALF], BF16, name="hidden")
            nc.vector.tensor_tensor(pair_order(hidden[u]), bank_order(b_banks[u]), pair_order(relus[u]), MULT)

        def turn(u):
            pairs = hidden[u][:].bitcast(F32)
            turned_banks[u] = psum_turned.tile([P, 2, C], F32, name="turned_bank")
            for v in range(2):
                nc.tensor.transpose(turned_banks[u][:, v, :], pairs[:, v * P : (v + 1) * P], identity[:])

        def empty_turned(u):
            turned[u] = work.tile([P, C, PACK], BF16, name="turned", align_bytes=64)
            nc.scalar.copy(
                turned[u][:].rearrange("p c t -> p (c t)").bitcast(F32).rearrange("p (c v) -> p c v", v=2),
                turned_banks[u][:].rearrange("p v c -> p c v"),
            )

        def quantise_hidden(u):
            hidden_codes[u] = work.tile([P, C], U32, name="hidden_codes", align_bytes=64)
            hidden_scales[u] = work.tile([P, C], U8, name="hidden_scales", align_bytes=64)
            nc.vector.quantize_mx(
                out=hidden_codes[u][:].bitcast(FP8X4),
                scales=hidden_scales[u][:],
                in_=turned[u][:].rearrange("p c t -> p (c t)"),
            )

        def multiply_second(u):
            e, g = u // PASSES, u % PASSES
            if g == 0:
                y_banks[e] = psum_second.tile([P, C], F32, name="y_bank")
            nc.tensor.matmul_mx(
                out=y_banks[e][:],
                lhsT=w2[:, u, :].bitcast(FP4X4),
                lhsT_scale=s2[:, u, :],
                rhs=hidden_codes[u][:].bitcast(FP8X4),
                rhs_scale=hidden_scales[u][:],
                start=(g == 0),
                stop=(g == PASSES - 1),
            )

        def take_out(e):
            y_copies[e] = work.tile([P, C], F32, name="y_copy")
            nc.scalar.copy(y_copies[e][:], y_banks[e][:])

        def send_back(e):
            nc.vector.tensor_tensor(
                result[:].indirect(slots_of(places, e)), y_copies[e][:], gates[:, e * C : (e + 1) * C], MULT
            )

        calls = (
            (multiply_a, 0, 0),
            (multiply_a, 0, 1),
            (rectify, 0, 0),
            (quantise_hidden, 2, 0),
            (multiply_b, 0, 0),
            (quantise_hidden, 2, 1),
            (take_out, 4, None),
            (turn, 1, 0),
            (turn, 1, 1),
            (multiply_b, 0, 1),
            (rectify, 0, 1),
            (empty_turned, 1, 0),
            (gate_hidden, 0, 0),
            (quantise_tokens, -1, None),
            (empty_turned, 1, 1),
            (multiply_second, 3, 1),
            (multiply_second, 2, 0),
            (gate_hidden, 0, 1),
            (send_back, 4, None),
        )
        longest_lag = max(lag for call, lag, g in calls)
        for step in range(E + longest_lag):
            for call, lag, g in calls:
                e = step - lag
                if 0 <= e < E and (call is not quantise_tokens or e > 0):
                    call(e if g is None else e * PASSES + g)
        nc.sync.dma_start(out, result[:])
